import numpy as np, ml_dtypes
CORES = [49,52,55,57,60,63,65,68,71,73,76,79]
N = 12
F = 64
def setup_inputs(rng):
    return {"x": rng.standard_normal((N, 128, N * F), dtype=np.float32).astype(ml_dtypes.bfloat16), "w": rng.standard_normal((N, 128, 128), dtype=np.float32).astype(ml_dtypes.bfloat16)}
def setup_inputs_big(rng):
    d = setup_inputs(rng)
    for k in ("x", "w"): d[k] = (d[k].astype(np.float32) * 1024.0).astype(d[k].dtype)
    return d
def setup_inputs_small(rng):
    d = setup_inputs(rng)
    for k in ("x", "w"): d[k] = (d[k].astype(np.float32) * (1 / 1024.0)).astype(d[k].dtype)
    return d
def setup_inputs_apart(rng):
    d = setup_inputs(rng)
    f = (10.0 ** rng.permutation(np.linspace(-1.5, 1.5, N))).astype(np.float32).reshape(N, 1, 1)
    for k in ("x", "w"): d[k] = (d[k].astype(np.float32) * f).astype(d[k].dtype)
    return d
def reference(x, w):
    X, W = x.astype(np.float64), w.astype(np.float64)
    s = X.sum(axis=0)
    o = np.concatenate([W[r].T @ s[:, F * r:F * r + F] for r in range(N)], axis=1).astype(ml_dtypes.bfloat16 if x.dtype != np.float64 else np.float64)
    return {"y": np.broadcast_to(o, (N,) + o.shape)}

@@ -1,0 +1,166 @@
+from concourse.bass import DstId, RemoteDMATransfer
+
+N = 12
+F = 64
+K = 128
+G = 2
+BG = N // G
+W = BG * F
+NS = 6
+
+SCRATCH = {
+    "wS": ("sbuf", [128, K], "bfloat16"),
+    "xS": ("sbuf", [128, N * F], "bfloat16"),
+    "yS": ("sbuf", [128, N * F], "bfloat16"),
+    "wbuf": ("sbuf", [128, BG * K], "bfloat16"),
+    "xin": ("sbuf", [128, NS * W], "bfloat16"),
+    "xm": ("sbuf", [128, W], "bfloat16"),
+    "obuf": ("sbuf", [128, W], "bfloat16"),
+}
+for _b in range(BG):
+    SCRATCH["ps%d" % _b] = ("psum", [128, 512], "float32")
+
+SEMAPHORES = ["wl", "xl", "snt", "wd", "wf", "xa", "xf", "cp", "st"] \
+    + ["ya%d" % _g for _g in range(G)] + ["mm%d" % _b for _b in range(BG)]
+
+
+def _bits(mask):
+    return [b for b in range(mask.bit_length()) if (mask >> b) & 1]
+
+
+def _mask(bits):
+    m = 0
+    for b in bits:
+        m |= 1 << b
+    return m
+
+
+def _dst(topo, c):
+    a = topo.addr(c)
+    return DstId(rid=a[0], pnc=a[1])
+
+
+def rank_program(g, core, T, topo):
+    cores = list(T.cores)
+    chips = sorted({topo.chip(c) for c in cores})
+    ch = topo.chip(core)
+    if ch not in chips:
+        return
+    every = range(topo.CORES_PER_CHIP * topo.CHIPS)
+    mate_of = {a: [b for b in chips if topo.mates(a, b)][0] for a in chips}
+
+    def workers(a):
+        far = [k for k in every if topo.chip(k) == mate_of[a]]
+        found = {}
+        for k in every:
+            if topo.chip(k) == a and k not in cores and all(topo.may_write(k, d) for d in far):
+                found.setdefault(topo.die(k), k)
+        return [found[d] for d in sorted(found)][:G]
+
+    plane = [b for b in chips if topo.same_plane(ch, b)]
+    srcs = [i for i in range(N) if topo.chip(cores[i]) in [ch] + plane]
+    sem = T.sem
+    rank = T.rank_of(core)
+
+    if rank is not None:
+        g.sync.dma_start(T.wS[:], T.w[:]).then_inc(sem.wl, 16)
+        g.sync.dma_start(T.xS[:], T.x[:]).then_inc(sem.xl, 16)
+        near = workers(ch)
+        away = [workers(b) for b in plane]
+        off = _bits(topo.mask(core, away[0][0]))
+        stay = [b for b in _bits(topo.mask(core, near[0])) if b not in off]
+        n_on = len(stay) // G
+        n_off = len(off) // (G * len(plane))
+        gr, slot = divmod(rank, BG)
+        me = srcs.index(rank)
+        tr = [RemoteDMATransfer(dst_ids=[_dst(topo, near[gr])], dma_engine_mask=_mask(stay[:n_on]), remote_sem=sem.wd,
+                                src=T.wS[:], dst=T.wbuf[:, slot * K:(slot + 1) * K])]
+        for j, ws in enumerate(away):
+            tr.append(RemoteDMATransfer(dst_ids=[_dst(topo, ws[gr])],
+                                        dma_engine_mask=_mask(off[j * n_off:(j + 1) * n_off]), remote_sem=sem.wd,
+                                        src=T.wS[:], dst=T.wbuf[:, slot * K:(slot + 1) * K]))
+        sent = n_on + n_off * len(away)
+        g.wait_ge(sem.wl, 16)
+        g.remote_dma_fused(tr, local_sem=sem.snt)
+        tr = []
+        for q in range(G):
+            tr.append(RemoteDMATransfer(dst_ids=[_dst(topo, near[q])],
+                                        dma_engine_mask=_mask(stay[q * n_on:(q + 1) * n_on]), remote_sem=sem.xa,
+                                        src=T.xS[:, q * W:(q + 1) * W], dst=T.xin[:, me * W:(me + 1) * W]))
+            sent += n_on
+            for j, ws in enumerate(away):
+                e = (j * G + q) * n_off
+                tr.append(RemoteDMATransfer(dst_ids=[_dst(topo, ws[q])], dma_engine_mask=_mask(off[e:e + n_off]),
+                                            remote_sem=sem.xa,
+                                            src=T.xS[:, q * W:(q + 1) * W], dst=T.xin[:, me * W:(me + 1) * W]))
+                sent += n_off
+        g.wait_ge(sem.xl, 16)
+        g.remote_dma_fused(tr, local_sem=sem.snt)
+        n_all = len(_bits(topo.mask(near[0], core)))
+        for q in range(G):
+            qu = g.sync if q % 2 == 0 else g.scalar
+            qu.wait_ge(sem["ya%d" % q], n_all)
+            qu.dma_start(T.y[:, q * W:(q + 1) * W], T.yS[:, q * W:(q + 1) * W]).then_inc(sem.st, 16)
+        g.wait_ge(sem.snt, sent)
+        g.wait_ge(sem.st, 16 * G)
+        return
+
+    mine = workers(ch)
+    if core not in mine:
+        return
+    q = mine.index(core)
+    twin = workers(mate_of[ch])[q]
+    link = topo.mask(core, twin)
+    n_link = len(_bits(link))
+    a = topo.addr(twin)
+    blocks = list(range(q * BG, (q + 1) * BG))
+    direct = [r - q * BG for r in blocks if r in srcs]
+    passed = [r - q * BG for r in blocks if r not in srcs]
+    lo, hi = min(direct), max(direct) + 1
+    assert hi - lo == len(direct)
+
+    def engines_from(i, what):
+        c = cores[i]
+        o = _bits(topo.mask(c, workers(plane[0])[0] if topo.chip(c) == ch else core))
+        if topo.chip(c) == ch:
+            return (len(_bits(topo.mask(c, core))) - len(o)) // G
+        return len(o) // (G * len(plane))
+
+    n_wd = sum(engines_from(q * BG + s, "w") for s in direct)
+    n_xa = sum(engines_from(i, "x") for i in srcs)
+
+    g.wait_ge(sem.wd, n_wd)
+    g.remote_dma(T.wbuf[:, lo * K:hi * K], T.wbuf[:, lo * K:hi * K], sem.wf, sem.snt, a[1], a[0], link)
+    g.wait_ge(sem.xa, n_xa)
+    g.remote_dma_fused([RemoteDMATransfer(dst_ids=[_dst(topo, twin)], dma_engine_mask=link, remote_sem=sem.xf,
+                                          srcs=[T.xin[:, i * W:(i + 1) * W] for i in range(NS)], dsts=[T.xm[:]],
+                                          alu_op=1)], local_sem=sem.snt)
+
+    def own(s):
+        for i in range(NS):
+            g.tensor.matmul(T["ps%d" % s][:, 0:F], T.wbuf[:, s * K:(s + 1) * K],
+                            T.xin[:, i * W + s * F:i * W + (s + 1) * F], start=(i == 0), stop=False)
+
+    g.tensor.wait_ge(sem.wd, n_wd)
+    g.tensor.wait_ge(sem.xa, n_xa)
+    for s in direct:
+        own(s)
+    g.tensor.wait_ge(sem.wf, n_link)
+    for s in passed:
+        own(s)
+    g.tensor.wait_ge(sem.xf, n_link)
+    for s in range(BG):
+        g.tensor.matmul(T["ps%d" % s][:, 0:F], T.wbuf[:, s * K:(s + 1) * K], T.xm[:, s * F:(s + 1) * F],
+                        start=False, stop=True).then_inc(sem["mm%d" % s], 1)
+    for s in range(BG):
+        g.vector.wait_ge(sem["mm%d" % s], 1)
+        g.vector.tensor_copy(T.obuf[:, s * F:(s + 1) * F], T["ps%d" % s][:, 0:F]).then_inc(sem.cp, 1)
+
+    home = [c for c in cores if topo.chip(c) == ch]
+    wide = topo.mask(core, home[0])
+    g.wait_ge(sem.cp, BG)
+    g.remote_dma_fused([RemoteDMATransfer(dst_ids=[_dst(topo, c) for c in home], dma_engine_mask=wide,
+                                          remote_sem=sem["ya%d" % q], srcs=[T.obuf[:]],
+                                          dsts=[T.yS[:, q * W:(q + 1) * W] for c in home], alu_op=0)],
+                       local_sem=sem.snt)
+    g.wait_ge(sem.snt, 2 * n_link + len(_bits(wide)))

@@ -3,8 +3,8 @@ from concourse.bass import DstId, RemoteDMATransfer
 N = 12
 F = 64
 K = 128
-G = 2
-BG = N // G
+BG = 3
+NG = N // BG
 W = BG * F
 NS = 6
 
@@ -13,6 +13,7 @@ SCRATCH = {
     "xS": ("sbuf", [128, N * F], "bfloat16"),
     "yS": ("sbuf", [128, N * F], "bfloat16"),
     "wbuf": ("sbuf", [128, BG * K], "bfloat16"),
+    "wrel": ("sbuf", [128, K], "bfloat16"),
     "xin": ("sbuf", [128, NS * W], "bfloat16"),
     "xm": ("sbuf", [128, W], "bfloat16"),
     "obuf": ("sbuf", [128, W], "bfloat16"),
@@ -20,8 +21,8 @@ SCRATCH = {
 for _b in range(BG):
     SCRATCH["ps%d" % _b] = ("psum", [128, 512], "float32")
 
-SEMAPHORES = ["wl", "xl", "snt", "wd", "wf", "xa", "xf", "cp", "st"] \
-    + ["ya%d" % _g for _g in range(G)] + ["mm%d" % _b for _b in range(BG)]
+SEMAPHORES = ["wl", "xl", "snt", "wd", "wr", "wf", "xa", "xf", "cp", "st"] \
+    + ["ya%d" % _g for _g in range(NG)] + ["mm%d" % _b for _b in range(BG)]
 
 
 def _bits(mask):
@@ -48,106 +49,109 @@ def rank_program(g, core, T, topo):
         return
     every = range(topo.CORES_PER_CHIP * topo.CHIPS)
     mate_of = {a: [b for b in chips if topo.mates(a, b)][0] for a in chips}
+    gchip = [topo.chip(cores[k * BG]) for k in range(NG)]
+    assert all(topo.chip(cores[i]) == gchip[i // BG] for i in range(N))
 
     def workers(a):
-        far = [k for k in every if topo.chip(k) == mate_of[a]]
+        far = [k for k in every if topo.chip(k) in chips and topo.chip(k) != a]
         found = {}
         for k in every:
             if topo.chip(k) == a and k not in cores and all(topo.may_write(k, d) for d in far):
                 found.setdefault(topo.die(k), k)
-        return [found[d] for d in sorted(found)][:G]
+        return [found[d] for d in sorted(found)][:2]
+
+    def widx(k):
+        return sorted([gchip[k], mate_of[gchip[k]]]).index(gchip[k])
+
+    def site(k, a):
+        for b in (gchip[k], mate_of[gchip[k]]):
+            if b == a or topo.same_plane(a, b):
+                return workers(b)[widx(k)]
 
     plane = [b for b in chips if topo.same_plane(ch, b)]
+    assert len(plane) == 1
     srcs = [i for i in range(N) if topo.chip(cores[i]) in [ch] + plane]
+    home = [c for c in cores if topo.chip(c) == ch]
+    away = [c for c in cores if topo.chip(c) == plane[0]]
+    near = workers(ch)
     sem = T.sem
     rank = T.rank_of(core)
+    on_chip = [c for c in home + near if c != core][0]
+    off = _bits(topo.mask(core, away[0]))
+    stay = [b for b in _bits(topo.mask(core, on_chip)) if b not in off]
+    n_on, n_off = len(stay) // 2, len(off) // 2
 
     if rank is not None:
         g.sync.dma_start(T.wS[:], T.w[:]).then_inc(sem.wl, 16)
         g.sync.dma_start(T.xS[:], T.x[:]).then_inc(sem.xl, 16)
-        near = workers(ch)
-        away = [workers(b) for b in plane]
-        off = _bits(topo.mask(core, away[0][0]))
-        stay = [b for b in _bits(topo.mask(core, near[0])) if b not in off]
-        n_on = len(stay) // G
-        n_off = len(off) // (G * len(plane))
-        gr, slot = divmod(rank, BG)
+        kown, slot = divmod(rank, BG)
         me = srcs.index(rank)
-        tr = [RemoteDMATransfer(dst_ids=[_dst(topo, near[gr])], dma_engine_mask=_mask(stay[:n_on]), remote_sem=sem.wd,
+        mine = site(kown, ch)
+        other = [c for c in near if c != mine][0]
+        tr = [RemoteDMATransfer(dst_ids=[_dst(topo, mine)], dma_engine_mask=_mask(stay[:n_on]), remote_sem=sem.wd,
                                 src=T.wS[:], dst=T.wbuf[:, slot * K:(slot + 1) * K])]
-        for j, ws in enumerate(away):
-            tr.append(RemoteDMATransfer(dst_ids=[_dst(topo, ws[gr])],
-                                        dma_engine_mask=_mask(off[j * n_off:(j + 1) * n_off]), remote_sem=sem.wd,
-                                        src=T.wS[:], dst=T.wbuf[:, slot * K:(slot + 1) * K]))
-        sent = n_on + n_off * len(away)
+        sent = n_on
+        if slot == BG - 1:
+            tr.append(RemoteDMATransfer(dst_ids=[_dst(topo, other)], dma_engine_mask=_mask(stay[n_on:2 * n_on]),
+                                        remote_sem=sem.wr, src=T.wS[:], dst=T.wrel[:]))
+            sent += n_on
         g.wait_ge(sem.wl, 16)
         g.remote_dma_fused(tr, local_sem=sem.snt)
         tr = []
-        for q in range(G):
-            tr.append(RemoteDMATransfer(dst_ids=[_dst(topo, near[q])],
-                                        dma_engine_mask=_mask(stay[q * n_on:(q + 1) * n_on]), remote_sem=sem.xa,
-                                        src=T.xS[:, q * W:(q + 1) * W], dst=T.xin[:, me * W:(me + 1) * W]))
-            sent += n_on
-            for j, ws in enumerate(away):
-                e = (j * G + q) * n_off
-                tr.append(RemoteDMATransfer(dst_ids=[_dst(topo, ws[q])], dma_engine_mask=_mask(off[e:e + n_off]),
-                                            remote_sem=sem.xa,
-                                            src=T.xS[:, q * W:(q + 1) * W], dst=T.xin[:, me * W:(me + 1) * W]))
-                sent += n_off
+        cnt = {True: 0, False: 0}
+        for k in range(NG):
+            s = site(k, ch)
+            here = topo.chip(s) == ch
+            j = cnt[here]
+            cnt[here] += 1
+            eng = stay[j * n_on:(j + 1) * n_on] if here else off[j * n_off:(j + 1) * n_off]
+            tr.append(RemoteDMATransfer(dst_ids=[_dst(topo, s)], dma_engine_mask=_mask(eng), remote_sem=sem.xa,
+                                        src=T.xS[:, k * W:(k + 1) * W], dst=T.xin[:, me * W:(me + 1) * W]))
+            sent += len(eng)
         g.wait_ge(sem.xl, 16)
         g.remote_dma_fused(tr, local_sem=sem.snt)
-        n_all = len(_bits(topo.mask(near[0], core)))
-        for q in range(G):
-            qu = g.sync if q % 2 == 0 else g.scalar
-            qu.wait_ge(sem["ya%d" % q], n_all)
-            qu.dma_start(T.y[:, q * W:(q + 1) * W], T.yS[:, q * W:(q + 1) * W]).then_inc(sem.st, 16)
+        for qu, b in ((g.sync, ch), (g.scalar, plane[0])):
+            ks = [k for k in range(NG) if topo.chip(site(k, ch)) == b]
+            assert ks == list(range(ks[0], ks[0] + len(ks)))
+            for k in ks:
+                qu.wait_ge(sem["ya%d" % k], len(stay) if b == ch else len(off))
+            qu.dma_start(T.y[:, ks[0] * W:(ks[-1] + 1) * W], T.yS[:, ks[0] * W:(ks[-1] + 1) * W]).then_inc(sem.st, 16)
         g.wait_ge(sem.snt, sent)
-        g.wait_ge(sem.st, 16 * G)
+        g.wait_ge(sem.st, 32)
         return
 
-    mine = workers(ch)
-    if core not in mine:
+    if core not in near:
         return
-    q = mine.index(core)
-    twin = workers(mate_of[ch])[q]
+    q = near.index(core)
+    k = [kk for kk in range(NG) if site(kk, ch) == core][0]
+    direct = gchip[k] == ch
+    far = workers(mate_of[ch])
+    twin = far[q]
     link = topo.mask(core, twin)
     n_link = len(_bits(link))
-    a = topo.addr(twin)
-    blocks = list(range(q * BG, (q + 1) * BG))
-    direct = [r - q * BG for r in blocks if r in srcs]
-    passed = [r - q * BG for r in blocks if r not in srcs]
-    lo, hi = min(direct), max(direct) + 1
-    assert hi - lo == len(direct)
+    n_xa = len(home) * n_on + len(away) * n_off
 
-    def engines_from(i, what):
-        c = cores[i]
-        o = _bits(topo.mask(c, workers(plane[0])[0] if topo.chip(c) == ch else core))
-        if topo.chip(c) == ch:
-            return (len(_bits(topo.mask(c, core))) - len(o)) // G
-        return len(o) // (G * len(plane))
-
-    n_wd = sum(engines_from(q * BG + s, "w") for s in direct)
-    n_xa = sum(engines_from(i, "x") for i in srcs)
-
-    g.wait_ge(sem.wd, n_wd)
-    g.remote_dma(T.wbuf[:, lo * K:hi * K], T.wbuf[:, lo * K:hi * K], sem.wf, sem.snt, a[1], a[0], link)
+    if direct:
+        a = topo.addr(twin)
+        n_w = BG * n_on
+        g.wait_ge(sem.wd, n_w)
+        g.remote_dma(T.wbuf[:, 0:(BG - 1) * K], T.wbuf[:, 0:(BG - 1) * K], sem.wf, sem.snt, a[1], a[0], link)
+        g.tensor.wait_ge(sem.wd, n_w)
+    else:
+        a = topo.addr(far[1 - q])
+        g.wait_ge(sem.wr, n_on)
+        g.remote_dma(T.wbuf[:, (BG - 1) * K:BG * K], T.wrel[:], sem.wf, sem.snt, a[1], a[0], link)
+        g.tensor.wait_ge(sem.wf, 2 * n_link)
     g.wait_ge(sem.xa, n_xa)
     g.remote_dma_fused([RemoteDMATransfer(dst_ids=[_dst(topo, twin)], dma_engine_mask=link, remote_sem=sem.xf,
                                           srcs=[T.xin[:, i * W:(i + 1) * W] for i in range(NS)], dsts=[T.xm[:]],
                                           alu_op=1)], local_sem=sem.snt)
 
-    def own(s):
+    g.tensor.wait_ge(sem.xa, n_xa)
+    for s in range(BG):
         for i in range(NS):
             g.tensor.matmul(T["ps%d" % s][:, 0:F], T.wbuf[:, s * K:(s + 1) * K],
                             T.xin[:, i * W + s * F:i * W + (s + 1) * F], start=(i == 0), stop=False)
-
-    g.tensor.wait_ge(sem.wd, n_wd)
-    g.tensor.wait_ge(sem.xa, n_xa)
-    for s in direct:
-        own(s)
-    g.tensor.wait_ge(sem.wf, n_link)
-    for s in passed:
-        own(s)
     g.tensor.wait_ge(sem.xf, n_link)
     for s in range(BG):
         g.tensor.matmul(T["ps%d" % s][:, 0:F], T.wbuf[:, s * K:(s + 1) * K], T.xm[:, s * F:(s + 1) * F],
@@ -156,11 +160,9 @@ def rank_program(g, core, T, topo):
         g.vector.wait_ge(sem["mm%d" % s], 1)
         g.vector.tensor_copy(T.obuf[:, s * F:(s + 1) * F], T["ps%d" % s][:, 0:F]).then_inc(sem.cp, 1)
 
-    home = [c for c in cores if topo.chip(c) == ch]
-    wide = topo.mask(core, home[0])
     g.wait_ge(sem.cp, BG)
-    g.remote_dma_fused([RemoteDMATransfer(dst_ids=[_dst(topo, c) for c in home], dma_engine_mask=wide,
-                                          remote_sem=sem["ya%d" % q], srcs=[T.obuf[:]],
-                                          dsts=[T.yS[:, q * W:(q + 1) * W] for c in home], alu_op=0)],
-                       local_sem=sem.snt)
-    g.wait_ge(sem.snt, 2 * n_link + len(_bits(wide)))
+    g.remote_dma_fused([RemoteDMATransfer(dst_ids=[_dst(topo, c) for c in grp], dma_engine_mask=_mask(eng),
+                                          remote_sem=sem["ya%d" % k], srcs=[T.obuf[:]],
+                                          dsts=[T.yS[:, k * W:(k + 1) * W] for c in grp], alu_op=0)
+                        for grp, eng in ((home, stay), (away, off))], local_sem=sem.snt)
+    g.wait_ge(sem.snt, 2 * n_link + len(stay) + len(off))

@@ -1,4 +1,5 @@
 from concourse.bass import DstId, RemoteDMATransfer
+from concourse.mybir import AluOpType
 
 N = 12
 F = 64
@@ -13,16 +14,19 @@ SCRATCH = {
     "xS": ("sbuf", [128, N * F], "bfloat16"),
     "yS": ("sbuf", [128, N * F], "bfloat16"),
     "wbuf": ("sbuf", [128, BG * K], "bfloat16"),
-    "wrel": ("sbuf", [128, K], "bfloat16"),
+    "wrel": ("sbuf", [128, BG * K], "bfloat16"),
+    "idm": ("sbuf", [128, K], "bfloat16"),
     "xin": ("sbuf", [128, NS * W], "bfloat16"),
+    "xs": ("sbuf", [128, W], "bfloat16"),
     "xm": ("sbuf", [128, W], "bfloat16"),
     "obuf": ("sbuf", [128, W], "bfloat16"),
+    "pss": ("psum", [128, 512], "float32"),
 }
 for _b in range(BG):
     SCRATCH["ps%d" % _b] = ("psum", [128, 512], "float32")
 
-SEMAPHORES = ["wl", "xl", "snt", "wd", "wr", "wf", "xa", "xf", "cp", "st"] \
-    + ["ya%d" % _g for _g in range(NG)] + ["mm%d" % _b for _b in range(BG)]
+SEMAPHORES = ["wl", "xl", "snt", "wd", "wr", "wf", "xf", "cp", "st", "on", "idn", "sm", "sc"] \
+    + ["ya%d" % _g for _g in range(NG)] + ["mm%d" % _b for _b in range(BG)] + ["xa%d" % _i for _i in range(NS)]
 
 
 def _bits(mask):
@@ -68,6 +72,20 @@ def rank_program(g, core, T, topo):
             if b == a or topo.same_plane(a, b):
                 return workers(b)[widx(k)]
 
+    def far_site(k):
+        return workers(mate_of[gchip[k]])[widx(k)]
+
+    def ways(k):
+        s = site(k, gchip[k])
+        relays = [s] + [c for c in workers(gchip[k]) if c != s]
+        out = []
+        for slot in range(BG):
+            if topo.may_write(cores[k * BG + slot], far_site(k)):
+                out.append(None)
+            else:
+                out.append(relays[len([v for v in out if v is not None]) % len(relays)])
+        return out
+
     plane = [b for b in chips if topo.same_plane(ch, b)]
     assert len(plane) == 1
     srcs = [i for i in range(N) if topo.chip(cores[i]) in [ch] + plane]
@@ -81,35 +99,38 @@ def rank_program(g, core, T, topo):
     stay = [b for b in _bits(topo.mask(core, on_chip)) if b not in off]
     n_on, n_off = len(stay) // 2, len(off) // 2
 
+    def w_eng(k, slot):
+        return len(off) if ways(k)[slot] == site(k, gchip[k]) else len(off) // 2
+
     if rank is not None:
         g.sync.dma_start(T.wS[:], T.w[:]).then_inc(sem.wl, 16)
-        g.sync.dma_start(T.xS[:], T.x[:]).then_inc(sem.xl, 16)
+        g.scalar.dma_start(T.xS[:], T.x[:]).then_inc(sem.xl, 16)
         kown, slot = divmod(rank, BG)
         me = srcs.index(rank)
         mine = site(kown, ch)
-        other = [c for c in near if c != mine][0]
-        tr = [RemoteDMATransfer(dst_ids=[_dst(topo, mine)], dma_engine_mask=_mask(stay[:n_on]), remote_sem=sem.wd,
-                                src=T.wS[:], dst=T.wbuf[:, slot * K:(slot + 1) * K])]
-        sent = n_on
-        if slot == BG - 1:
-            tr.append(RemoteDMATransfer(dst_ids=[_dst(topo, other)], dma_engine_mask=_mask(stay[n_on:2 * n_on]),
-                                        remote_sem=sem.wr, src=T.wS[:], dst=T.wrel[:]))
-            sent += n_on
+        way = ways(kown)[slot]
+        col = slice(slot * K, (slot + 1) * K)
+        if way == mine:
+            to = [(mine, T.wbuf[:, col], sem.wr)]
+        elif way is None:
+            to = [(mine, T.wbuf[:, col], sem.wd), (far_site(kown), T.wbuf[:, col], sem.wf)]
+        else:
+            to = [(mine, T.wbuf[:, col], sem.wd), (way, T.wrel[:, col], sem.wr)]
+        ne = w_eng(kown, slot)
         g.wait_ge(sem.wl, 16)
-        g.remote_dma_fused(tr, local_sem=sem.snt)
-        tr = []
-        cnt = {True: 0, False: 0}
-        for k in range(NG):
-            s = site(k, ch)
-            here = topo.chip(s) == ch
-            j = cnt[here]
-            cnt[here] += 1
-            eng = stay[j * n_on:(j + 1) * n_on] if here else off[j * n_off:(j + 1) * n_off]
-            tr.append(RemoteDMATransfer(dst_ids=[_dst(topo, s)], dma_engine_mask=_mask(eng), remote_sem=sem.xa,
-                                        src=T.xS[:, k * W:(k + 1) * W], dst=T.xin[:, me * W:(me + 1) * W]))
-            sent += len(eng)
+        g.remote_dma_fused([RemoteDMATransfer(dst_ids=[_dst(topo, c)], dma_engine_mask=_mask(off[j * ne:(j + 1) * ne]),
+                                              remote_sem=s, src=T.wS[:], dst=ap)
+                            for j, (c, ap, s) in enumerate(to)], local_sem=sem.snt)
+        sent = ne * len(to)
         g.wait_ge(sem.xl, 16)
-        g.remote_dma_fused(tr, local_sem=sem.snt)
+        for here, eng, n_e in ((False, off, n_off), (True, stay, n_on)):
+            ks = [k for k in range(NG) if (topo.chip(site(k, ch)) == ch) == here]
+            g.remote_dma_fused([RemoteDMATransfer(dst_ids=[_dst(topo, site(k, ch))],
+                                                  dma_engine_mask=_mask(eng[j * n_e:(j + 1) * n_e]),
+                                                  remote_sem=sem["xa%d" % me], src=T.xS[:, k * W:(k + 1) * W],
+                                                  dst=T.xin[:, me * W:(me + 1) * W])
+                                for j, k in enumerate(ks)], local_sem=sem.snt)
+            sent += n_e * len(ks)
         for qu, b in ((g.sync, ch), (g.scalar, plane[0])):
             ks = [k for k in range(NG) if topo.chip(site(k, ch)) == b]
             assert ks == list(range(ks[0], ks[0] + len(ks)))
@@ -125,33 +146,49 @@ def rank_program(g, core, T, topo):
     q = near.index(core)
     k = [kk for kk in range(NG) if site(kk, ch) == core][0]
     direct = gchip[k] == ch
-    far = workers(mate_of[ch])
-    twin = far[q]
+    twin = workers(mate_of[ch])[q]
     link = topo.mask(core, twin)
     n_link = len(_bits(link))
-    n_xa = len(home) * n_on + len(away) * n_off
+    own = gchip.index(ch)
+    pass_on = [s for s in range(BG) if ways(own)[s] == core]
+    n_wr = sum(w_eng(own, s) for s in pass_on)
+
+    g.vector.memset(T.idm[:], 1.0).then_inc(sem.on, 1)
+    g.wait_ge(sem.on, 1)
+    g.affine_select(T.idm[:], T.idm[:], [[-1, K]], AluOpType.is_equal, 0.0, 0, 1).then_inc(sem.idn, 1)
+    a = topo.addr(far_site(own))
+    if pass_on:
+        g.wait_ge(sem.wr, n_wr)
+    for s in pass_on:
+        g.remote_dma(T.wbuf[:, s * K:(s + 1) * K], (T.wbuf if direct else T.wrel)[:, s * K:(s + 1) * K],
+                     sem.wf, sem.snt, a[1], a[0], link)
+
+    def crowd(c):
+        return len([d for d in cores if topo.chip(d) == topo.chip(c) and topo.die(d) == topo.die(c)])
+
+    order = [i for i in range(NS) if cores[srcs[i]] in home] \
+        + sorted([i for i in range(NS) if cores[srcs[i]] in away], key=lambda i: crowd(cores[srcs[i]]))
+    g.tensor.wait_ge(sem.idn, 1)
+    for n, i in enumerate(order):
+        g.tensor.wait_ge(sem["xa%d" % i], n_on if cores[srcs[i]] in home else n_off)
+        mm = g.tensor.matmul(T.pss[:, 0:W], T.idm[:], T.xin[:, i * W:(i + 1) * W], start=(n == 0), stop=(n == NS - 1))
+    mm.then_inc(sem.sm, 1)
+    g.vector.wait_ge(sem.sm, 1)
+    g.vector.tensor_copy(T.xs[:], T.pss[:, 0:W]).then_inc(sem.sc, 1)
+    a = topo.addr(twin)
+    g.wait_ge(sem.sc, 1)
+    g.remote_dma(T.xm[:], T.xs[:], sem.xf, sem.snt, a[1], a[0], link)
 
     if direct:
-        a = topo.addr(twin)
-        n_w = BG * n_on
-        g.wait_ge(sem.wd, n_w)
-        g.remote_dma(T.wbuf[:, 0:(BG - 1) * K], T.wbuf[:, 0:(BG - 1) * K], sem.wf, sem.snt, a[1], a[0], link)
-        g.tensor.wait_ge(sem.wd, n_w)
+        if pass_on:
+            g.tensor.wait_ge(sem.wr, n_wr)
+        g.tensor.wait_ge(sem.wd, sum(w_eng(k, s) for s in range(BG) if s not in pass_on))
     else:
-        a = topo.addr(far[1 - q])
-        g.wait_ge(sem.wr, n_on)
-        g.remote_dma(T.wbuf[:, (BG - 1) * K:BG * K], T.wrel[:], sem.wf, sem.snt, a[1], a[0], link)
-        g.tensor.wait_ge(sem.wf, 2 * n_link)
-    g.wait_ge(sem.xa, n_xa)
-    g.remote_dma_fused([RemoteDMATransfer(dst_ids=[_dst(topo, twin)], dma_engine_mask=link, remote_sem=sem.xf,
-                                          srcs=[T.xin[:, i * W:(i + 1) * W] for i in range(NS)], dsts=[T.xm[:]],
-                                          alu_op=1)], local_sem=sem.snt)
-
-    g.tensor.wait_ge(sem.xa, n_xa)
+        g.tensor.wait_ge(sem.wf, sum(w_eng(k, s) if ways(k)[s] is None else n_link for s in range(BG)))
+    g.tensor.wait_ge(sem.sc, 1)
     for s in range(BG):
-        for i in range(NS):
-            g.tensor.matmul(T["ps%d" % s][:, 0:F], T.wbuf[:, s * K:(s + 1) * K],
-                            T.xin[:, i * W + s * F:i * W + (s + 1) * F], start=(i == 0), stop=False)
+        g.tensor.matmul(T["ps%d" % s][:, 0:F], T.wbuf[:, s * K:(s + 1) * K], T.xs[:, s * F:(s + 1) * F],
+                        start=True, stop=False)
     g.tensor.wait_ge(sem.xf, n_link)
     for s in range(BG):
         g.tensor.matmul(T["ps%d" % s][:, 0:F], T.wbuf[:, s * K:(s + 1) * K], T.xm[:, s * F:(s + 1) * F],
@@ -161,8 +198,9 @@ def rank_program(g, core, T, topo):
         g.vector.tensor_copy(T.obuf[:, s * F:(s + 1) * F], T["ps%d" % s][:, 0:F]).then_inc(sem.cp, 1)
 
     g.wait_ge(sem.cp, BG)
-    g.remote_dma_fused([RemoteDMATransfer(dst_ids=[_dst(topo, c) for c in grp], dma_engine_mask=_mask(eng),
-                                          remote_sem=sem["ya%d" % k], srcs=[T.obuf[:]],
-                                          dsts=[T.yS[:, k * W:(k + 1) * W] for c in grp], alu_op=0)
-                        for grp, eng in ((home, stay), (away, off))], local_sem=sem.snt)
-    g.wait_ge(sem.snt, 2 * n_link + len(stay) + len(off))
+    for grp, eng in ((away, off), (home, stay)):
+        g.remote_dma_fused([RemoteDMATransfer(dst_ids=[_dst(topo, c) for c in grp], dma_engine_mask=_mask(eng),
+                                              remote_sem=sem["ya%d" % k], srcs=[T.obuf[:]],
+                                              dsts=[T.yS[:, k * W:(k + 1) * W] for c in grp], alu_op=0)],
+                           local_sem=sem.snt)
+    g.wait_ge(sem.snt, n_link * (len(pass_on) + 1) + len(stay) + len(off))

from concourse.bass import DstId, RemoteDMATransfer
from concourse.mybir import AluOpType

N = 12
F = 64
K = 128
BG = 3
NG = N // BG
W = BG * F
NS = 6

SCRATCH = {
    "wS": ("sbuf", [128, K], "bfloat16"),
    "xS": ("sbuf", [128, N * F], "bfloat16"),
    "yS": ("sbuf", [128, N * F], "bfloat16"),
    "wbuf": ("sbuf", [128, BG * K], "bfloat16"),
    "wrel": ("sbuf", [128, BG * K], "bfloat16"),
    "idm": ("sbuf", [128, K], "bfloat16"),
    "xin": ("sbuf", [128, NS * W], "bfloat16"),
    "xs": ("sbuf", [128, W], "bfloat16"),
    "xm": ("sbuf", [128, W], "bfloat16"),
    "obuf": ("sbuf", [128, W], "bfloat16"),
    "pss": ("psum", [128, 512], "float32"),
}
for _b in range(BG):
    SCRATCH["ps%d" % _b] = ("psum", [128, 512], "float32")

SEMAPHORES = ["wl", "xl", "snt", "wd", "wr", "wf", "xf", "cp", "st", "on", "idn", "sm", "sc"] \
    + ["ya%d" % _g for _g in range(NG)] + ["mm%d" % _b for _b in range(BG)] + ["xa%d" % _i for _i in range(NS)]


def _bits(mask):
    return [b for b in range(mask.bit_length()) if (mask >> b) & 1]


def _mask(bits):
    m = 0
    for b in bits:
        m |= 1 << b
    return m


def _dst(topo, c):
    a = topo.addr(c)
    return DstId(rid=a[0], pnc=a[1])


def rank_program(g, core, T, topo):
    cores = list(T.cores)
    chips = sorted({topo.chip(c) for c in cores})
    ch = topo.chip(core)
    if ch not in chips:
        return
    every = range(topo.CORES_PER_CHIP * topo.CHIPS)
    mate_of = {a: [b for b in chips if topo.mates(a, b)][0] for a in chips}
    gchip = [topo.chip(cores[k * BG]) for k in range(NG)]
    assert all(topo.chip(cores[i]) == gchip[i // BG] for i in range(N))

    def workers(a):
        far = [k for k in every if topo.chip(k) in chips and topo.chip(k) != a]
        found = {}
        for k in every:
            if topo.chip(k) == a and k not in cores and all(topo.may_write(k, d) for d in far):
                found.setdefault(topo.die(k), k)
        return [found[d] for d in sorted(found)][:2]

    def widx(k):
        return sorted([gchip[k], mate_of[gchip[k]]]).index(gchip[k])

    def site(k, a):
        for b in (gchip[k], mate_of[gchip[k]]):
            if b == a or topo.same_plane(a, b):
                return workers(b)[widx(k)]

    def far_site(k):
        return workers(mate_of[gchip[k]])[widx(k)]

    def ways(k):
        s = site(k, gchip[k])
        relays = [s] + [c for c in workers(gchip[k]) if c != s]
        out = []
        for slot in range(BG):
            if topo.may_write(cores[k * BG + slot], far_site(k)):
                out.append(None)
            else:
                out.append(relays[len([v for v in out if v is not None]) % len(relays)])
        return out

    plane = [b for b in chips if topo.same_plane(ch, b)]
    assert len(plane) == 1
    srcs = [i for i in range(N) if topo.chip(cores[i]) in [ch] + plane]
    home = [c for c in cores if topo.chip(c) == ch]
    away = [c for c in cores if topo.chip(c) == plane[0]]
    near = workers(ch)
    sem = T.sem
    rank = T.rank_of(core)
    on_chip = [c for c in home + near if c != core][0]
    off = _bits(topo.mask(core, away[0]))
    stay = [b for b in _bits(topo.mask(core, on_chip)) if b not in off]
    n_on, n_off = len(stay) // 2, len(off) // 2

    def w_eng(k, slot):
        return len(off) if ways(k)[slot] == site(k, gchip[k]) else len(off) // 2

    if rank is not None:
        g.sync.dma_start(T.wS[:], T.w[:]).then_inc(sem.wl, 16)
        g.scalar.dma_start(T.xS[:], T.x[:]).then_inc(sem.xl, 16)
        kown, slot = divmod(rank, BG)
        me = srcs.index(rank)
        mine = site(kown, ch)
        way = ways(kown)[slot]
        col = slice(slot * K, (slot + 1) * K)
        if way == mine:
            to = [(mine, T.wbuf[:, col], sem.wr)]
        elif way is None:
            to = [(mine, T.wbuf[:, col], sem.wd), (far_site(kown), T.wbuf[:, col], sem.wf)]
        else:
            to = [(mine, T.wbuf[:, col], sem.wd), (way, T.wrel[:, col], sem.wr)]
        ne = w_eng(kown, slot)
        g.wait_ge(sem.wl, 16)
        g.remote_dma_fused([RemoteDMATransfer(dst_ids=[_dst(topo, c)], dma_engine_mask=_mask(off[j * ne:(j + 1) * ne]),
                                              remote_sem=s, src=T.wS[:], dst=ap)
                            for j, (c, ap, s) in enumerate(to)], local_sem=sem.snt)
        sent = ne * len(to)
        g.wait_ge(sem.xl, 16)
        for here, eng, n_e in ((False, off, n_off), (True, stay, n_on)):
            ks = [k for k in range(NG) if (topo.chip(site(k, ch)) == ch) == here]
            g.remote_dma_fused([RemoteDMATransfer(dst_ids=[_dst(topo, site(k, ch))],
                                                  dma_engine_mask=_mask(eng[j * n_e:(j + 1) * n_e]),
                                                  remote_sem=sem["xa%d" % me], src=T.xS[:, k * W:(k + 1) * W],
                                                  dst=T.xin[:, me * W:(me + 1) * W])
                                for j, k in enumerate(ks)], local_sem=sem.snt)
            sent += n_e * len(ks)
        for qu, b in ((g.sync, ch), (g.scalar, plane[0])):
            ks = [k for k in range(NG) if topo.chip(site(k, ch)) == b]
            assert ks == list(range(ks[0], ks[0] + len(ks)))
            for k in ks:
                qu.wait_ge(sem["ya%d" % k], len(stay) if b == ch else len(off))
            qu.dma_start(T.y[:, ks[0] * W:(ks[-1] + 1) * W], T.yS[:, ks[0] * W:(ks[-1] + 1) * W]).then_inc(sem.st, 16)
        g.wait_ge(sem.snt, sent)
        g.wait_ge(sem.st, 32)
        return

    if core not in near:
        return
    q = near.index(core)
    k = [kk for kk in range(NG) if site(kk, ch) == core][0]
    direct = gchip[k] == ch
    twin = workers(mate_of[ch])[q]
    link = topo.mask(core, twin)
    n_link = len(_bits(link))
    own = gchip.index(ch)
    pass_on = [s for s in range(BG) if ways(own)[s] == core]
    n_wr = sum(w_eng(own, s) for s in pass_on)

    g.vector.memset(T.idm[:], 1.0).then_inc(sem.on, 1)
    g.wait_ge(sem.on, 1)
    g.affine_select(T.idm[:], T.idm[:], [[-1, K]], AluOpType.is_equal, 0.0, 0, 1).then_inc(sem.idn, 1)
    a = topo.addr(far_site(own))
    if pass_on:
        g.wait_ge(sem.wr, n_wr)
    for s in pass_on:
        g.remote_dma(T.wbuf[:, s * K:(s + 1) * K], (T.wbuf if direct else T.wrel)[:, s * K:(s + 1) * K],
                     sem.wf, sem.snt, a[1], a[0], link)

    def crowd(c):
        return len([d for d in cores if topo.chip(d) == topo.chip(c) and topo.die(d) == topo.die(c)])

    order = [i for i in range(NS) if cores[srcs[i]] in home] \
        + sorted([i for i in range(NS) if cores[srcs[i]] in away], key=lambda i: crowd(cores[srcs[i]]))
    g.tensor.wait_ge(sem.idn, 1)
    for n, i in enumerate(order):
        g.tensor.wait_ge(sem["xa%d" % i], n_on if cores[srcs[i]] in home else n_off)
        mm = g.tensor.matmul(T.pss[:, 0:W], T.idm[:], T.xin[:, i * W:(i + 1) * W], start=(n == 0), stop=(n == NS - 1))
    mm.then_inc(sem.sm, 1)
    g.vector.wait_ge(sem.sm, 1)
    g.vector.tensor_copy(T.xs[:], T.pss[:, 0:W]).then_inc(sem.sc, 1)
    a = topo.addr(twin)
    g.wait_ge(sem.sc, 1)
    g.remote_dma(T.xm[:], T.xs[:], sem.xf, sem.snt, a[1], a[0], link)

    if direct:
        if pass_on:
            g.tensor.wait_ge(sem.wr, n_wr)
        g.tensor.wait_ge(sem.wd, sum(w_eng(k, s) for s in range(BG) if s not in pass_on))
    else:
        g.tensor.wait_ge(sem.wf, sum(w_eng(k, s) if ways(k)[s] is None else n_link for s in range(BG)))
    g.tensor.wait_ge(sem.sc, 1)
    for s in range(BG):
        g.tensor.matmul(T["ps%d" % s][:, 0:F], T.wbuf[:, s * K:(s + 1) * K], T.xs[:, s * F:(s + 1) * F],
                        start=True, stop=False)
    g.tensor.wait_ge(sem.xf, n_link)
    for s in range(BG):
        g.tensor.matmul(T["ps%d" % s][:, 0:F], T.wbuf[:, s * K:(s + 1) * K], T.xm[:, s * F:(s + 1) * F],
                        start=False, stop=True).then_inc(sem["mm%d" % s], 1)
    for s in range(BG):
        g.vector.wait_ge(sem["mm%d" % s], 1)
        g.vector.tensor_copy(T.obuf[:, s * F:(s + 1) * F], T["ps%d" % s][:, 0:F]).then_inc(sem.cp, 1)

    g.wait_ge(sem.cp, BG)
    for grp, eng in ((away, off), (home, stay)):
        g.remote_dma_fused([RemoteDMATransfer(dst_ids=[_dst(topo, c) for c in grp], dma_engine_mask=_mask(eng),
                                              remote_sem=sem["ya%d" % k], srcs=[T.obuf[:]],
                                              dsts=[T.yS[:, k * W:(k + 1) * W] for c in grp], alu_op=0)],
                           local_sem=sem.snt)
    g.wait_ge(sem.snt, n_link * (len(pass_on) + 1) + len(stay) + len(off))
